import numpy as np
import ml_dtypes

BF16 = ml_dtypes.bfloat16


def bf(x):
    return np.asarray(x, np.float32).astype(BF16)


def f32(x):
    return np.asarray(x, np.float32)


def f64(x):
    return np.asarray(x).astype(np.float64)


def striped(idx):
    return np.tile(idx.reshape(-1, 16).T, (8, 1))


S, K, M, N, E, Q = 512, 128, 256, 384, 4, 96


def setup_inputs():
    return {"base": bf(np.random.standard_normal((M, S))), "x": bf(np.random.standard_normal((K, N))), "w": bf(np.random.standard_normal((E, K, M)) / np.sqrt(K)), "c": f32(0.2 + 0.8 * np.random.random_sample((1, S))), "offs": striped(np.random.permutation(S)[:N])}


def reference(base, x, w, c, offs):
    idx = offs[:16].T.reshape(-1)
    z = f64(base).copy()
    for e in range(E):
        z[:, idx[e * Q : (e + 1) * Q]] = f64(w)[e].T @ f64(x)[:, e * Q : (e + 1) * Q]
    return z * f64(c)

@@ -1,0 +1,60 @@
+import concourse.mybir as mybir
+from concourse.masks import make_identity
+
+BF16, F32, U16 = mybir.dt.bfloat16, mybir.dt.float32, mybir.dt.uint16
+
+P = 128
+S = 512
+M = 256
+N = 384
+E = 4
+Q = N // E
+QC = Q // 16
+BLOCKS = M // P
+
+FLOPS = 2 * P * M * N
+
+
+def tile_scatter_matmul_kernel(tc, base, x, w, c, offs, out):
+    nc = tc.nc
+    with (
+        tc.tile_pool(name="held", bufs=1) as held,
+        tc.psum_pool(name="windows", bufs=1) as windows,
+    ):
+        offsets = held.tile([P, N // 16], U16, name="offsets")
+        nc.sync.dma_start(offsets[:], offs)
+
+        base_tiles = [held.tile([P, S], BF16, name=f"base{b}") for b in range(BLOCKS)]
+        nc.sync.dma_start(base_tiles[0][:], base[0:P, :])
+        nc.scalar.dma_start(base_tiles[1][:], base[P : 2 * P, :])
+
+        x_tile = held.tile([P, N], BF16, name="x_tile")
+        nc.scalar.dma_start(x_tile[:], x)
+        w_tile = held.tile([P, E, M], BF16, name="w_tile")
+        nc.gpsimd.dma_start(w_tile[:], w.rearrange("e k m -> k e m"))
+
+        c_tile = held.tile([P, S], F32, name="c_tile")
+        nc.gpsimd.dma_start(c_tile[:], c.broadcast_to([P, S]))
+
+        ident = held.tile([P, P], BF16, name="ident")
+        make_identity(nc, ident[:])
+
+        window_tiles = [windows.tile([P, S], F32, name=f"window{b}") for b in range(BLOCKS)]
+        for b in range(BLOCKS):
+            nc.tensor.matmul(window_tiles[b][:], ident[:], base_tiles[b][:], start=True, stop=True)
+
+        for b in range(BLOCKS):
+            for e in range(E):
+                nc.tensor.matmul(
+                    window_tiles[b][:].indirect(offsets[:, e * QC : (e + 1) * QC]),
+                    w_tile[:, e, b * P : (b + 1) * P],
+                    x_tile[:, e * Q : (e + 1) * Q],
+                    start=True,
+                    stop=True,
+                )
+
+        for b in range(BLOCKS):
+            scaled = held.tile([P, S], F32, name=f"scaled{b}")
+            nc.vector.tensor_tensor(scaled[:], window_tiles[b][:], c_tile[:], mybir.AluOpType.mult)
+            store_queue = nc.sync if b == 0 else nc.scalar
+            store_queue.dma_start(out[b * P : (b + 1) * P, :], scaled[:])

@@ -11,6 +11,7 @@ E = 4
 Q = N // E
 QC = Q // 16
 BLOCKS = M // P
+WARM_MATMULS = 3
 
 FLOPS = 2 * P * M * N
 
@@ -31,10 +32,16 @@ def tile_scatter_matmul_kernel(tc, base, x, w, c, offs, out):
         x_tile = held.tile([P, N], BF16, name="x_tile")
         nc.scalar.dma_start(x_tile[:], x)
         w_tile = held.tile([P, E, M], BF16, name="w_tile")
-        nc.gpsimd.dma_start(w_tile[:], w.rearrange("e k m -> k e m"))
+        nc.sync.dma_start(w_tile[:], w.rearrange("e k m -> k e m"))
 
         c_tile = held.tile([P, S], F32, name="c_tile")
-        nc.gpsimd.dma_start(c_tile[:], c.broadcast_to([P, S]))
+        nc.scalar.dma_start(c_tile[:], c.broadcast_to([P, S]))
+
+        zeros = held.tile([P, S], BF16, name="zeros")
+        nc.vector.memset(zeros[:], 0.0)
+        warm = windows.tile([P, S], F32, name="warm")
+        for i in range(WARM_MATMULS):
+            nc.tensor.matmul(warm[:], zeros[:, 0:P], zeros[:], start=True, stop=True)
 
         ident = held.tile([P, P], BF16, name="ident")
         make_identity(nc, ident[:])

@@ -25,6 +25,9 @@ def tile_scatter_matmul_kernel(tc, base, x, w, c, offs, out):
         offsets = held.tile([P, N // 16], U16, name="offsets")
         nc.sync.dma_start(offsets[:], offs)
 
+        c_row = held.tile([1, S], F32, name="c_row")
+        nc.scalar.dma_start(c_row[:], c)
+
         base_tiles = [held.tile([P, S], BF16, name=f"base{b}") for b in range(BLOCKS)]
         nc.sync.dma_start(base_tiles[0][:], base[0:P, :])
         nc.scalar.dma_start(base_tiles[1][:], base[P : 2 * P, :])
@@ -34,14 +37,18 @@ def tile_scatter_matmul_kernel(tc, base, x, w, c, offs, out):
         w_tile = held.tile([P, E, M], BF16, name="w_tile")
         nc.sync.dma_start(w_tile[:], w.rearrange("e k m -> k e m"))
 
-        c_tile = held.tile([P, S], F32, name="c_tile")
-        nc.scalar.dma_start(c_tile[:], c.broadcast_to([P, S]))
-
         zeros = held.tile([P, S], BF16, name="zeros")
         nc.vector.memset(zeros[:], 0.0)
         warm = windows.tile([P, S], F32, name="warm")
         for i in range(WARM_MATMULS):
             nc.tensor.matmul(warm[:], zeros[:, 0:P], zeros[:], start=True, stop=True)
+
+        ones_row = held.tile([1, P], F32, name="ones_row")
+        nc.vector.memset(ones_row[:], 1.0)
+        c_bank = windows.tile([P, S], F32, name="c_bank")
+        nc.tensor.matmul(c_bank[:], ones_row[:], c_row[:], start=True, stop=True)
+        c_tile = held.tile([P, S], F32, name="c_tile")
+        nc.vector.tensor_copy(c_tile[:], c_bank[:])
 
         ident = held.tile([P, P], BF16, name="ident")
         make_identity(nc, ident[:])

@@ -12,6 +12,7 @@ Q = N // E
 QC = Q // 16
 BLOCKS = M // P
 WARM_MATMULS = 3
+CPP = S // P
 
 FLOPS = 2 * P * M * N
 
@@ -25,8 +26,8 @@ def tile_scatter_matmul_kernel(tc, base, x, w, c, offs, out):
         offsets = held.tile([P, N // 16], U16, name="offsets")
         nc.sync.dma_start(offsets[:], offs)
 
-        c_row = held.tile([1, S], F32, name="c_row")
-        nc.scalar.dma_start(c_row[:], c)
+        c_cols = held.tile([P, CPP], F32, name="c_cols")
+        nc.scalar.dma_start(c_cols[:], c.rearrange("o (p a) -> p (o a)", p=P))
 
         base_tiles = [held.tile([P, S], BF16, name=f"base{b}") for b in range(BLOCKS)]
         nc.sync.dma_start(base_tiles[0][:], base[0:P, :])
@@ -43,15 +44,17 @@ def tile_scatter_matmul_kernel(tc, base, x, w, c, offs, out):
         for i in range(WARM_MATMULS):
             nc.tensor.matmul(warm[:], zeros[:, 0:P], zeros[:], start=True, stop=True)
 
-        ones_row = held.tile([1, P], F32, name="ones_row")
-        nc.vector.memset(ones_row[:], 1.0)
-        c_bank = windows.tile([P, S], F32, name="c_bank")
-        nc.tensor.matmul(c_bank[:], ones_row[:], c_row[:], start=True, stop=True)
-        c_tile = held.tile([P, S], F32, name="c_tile")
-        nc.vector.tensor_copy(c_tile[:], c_bank[:])
-
         ident = held.tile([P, P], BF16, name="ident")
         make_identity(nc, ident[:])
+        ident_f32 = held.tile([P, P], F32, name="ident_f32")
+        make_identity(nc, ident_f32[:])
+
+        c_bank = windows.tile([P, S], F32, name="c_bank")
+        c_bank_by_a = c_bank[:].rearrange("q (p a) -> q a p", a=CPP)
+        for a in range(CPP):
+            nc.tensor.transpose(c_bank_by_a[:, a, :], c_cols[:, a : a + 1].to_broadcast([P, P]), ident_f32[:])
+        c_tile = held.tile([P, S], F32, name="c_tile")
+        nc.vector.tensor_copy(c_tile[:], c_bank[:])
 
         window_tiles = [windows.tile([P, S], F32, name=f"window{b}") for b in range(BLOCKS)]
         for b in range(BLOCKS):

@@ -11,7 +11,7 @@ E = 4
 Q = N // E
 QC = Q // 16
 BLOCKS = M // P
-WARM_MATMULS = 3
+WARM_MATMULS = 4
 CPP = S // P
 
 FLOPS = 2 * P * M * N
@@ -38,11 +38,13 @@ def tile_scatter_matmul_kernel(tc, base, x, w, c, offs, out):
         w_tile = held.tile([P, E, M], BF16, name="w_tile")
         nc.sync.dma_start(w_tile[:], w.rearrange("e k m -> k e m"))
 
-        zeros = held.tile([P, S], BF16, name="zeros")
-        nc.vector.memset(zeros[:], 0.0)
+        zeros = held.tile([P, 1], BF16, name="zeros")
+        nc.gpsimd.memset(zeros[:], 0.0)
         warm = windows.tile([P, S], F32, name="warm")
         for i in range(WARM_MATMULS):
-            nc.tensor.matmul(warm[:], zeros[:, 0:P], zeros[:], start=True, stop=True)
+            nc.tensor.matmul(
+                warm[:], zeros[:].to_broadcast([P, P]), zeros[:].to_broadcast([P, S]), start=True, stop=True
+            )
 
         ident = held.tile([P, P], BF16, name="ident")
         make_identity(nc, ident[:])
@@ -50,11 +52,14 @@ def tile_scatter_matmul_kernel(tc, base, x, w, c, offs, out):
         make_identity(nc, ident_f32[:])
 
         c_bank = windows.tile([P, S], F32, name="c_bank")
-        c_bank_by_a = c_bank[:].rearrange("q (p a) -> q a p", a=CPP)
         for a in range(CPP):
-            nc.tensor.transpose(c_bank_by_a[:, a, :], c_cols[:, a : a + 1].to_broadcast([P, P]), ident_f32[:])
+            nc.tensor.transpose(
+                c_bank[:, a * P : (a + 1) * P], c_cols[:, a : a + 1].to_broadcast([P, P]), ident_f32[:]
+            )
         c_tile = held.tile([P, S], F32, name="c_tile")
-        nc.vector.tensor_copy(c_tile[:], c_bank[:])
+        nc.vector.tensor_copy(
+            c_tile[:].rearrange("q (p a) -> q p a", a=CPP), c_bank[:].rearrange("q (a p) -> q p a", a=CPP)
+        )
 
         window_tiles = [windows.tile([P, S], F32, name=f"window{b}") for b in range(BLOCKS)]
         for b in range(BLOCKS):

@@ -23,20 +23,21 @@ def tile_scatter_matmul_kernel(tc, base, x, w, c, offs, out):
         tc.tile_pool(name="held", bufs=1) as held,
         tc.psum_pool(name="windows", bufs=1) as windows,
     ):
+
+        c_cols = held.tile([P, CPP], F32, name="c_cols")
+        nc.sync.dma_start(c_cols[:], c.rearrange("o (p a) -> p (o a)", p=P))
+
         offsets = held.tile([P, N // 16], U16, name="offsets")
         nc.sync.dma_start(offsets[:], offs)
 
-        c_cols = held.tile([P, CPP], F32, name="c_cols")
-        nc.scalar.dma_start(c_cols[:], c.rearrange("o (p a) -> p (o a)", p=P))
-
         base_tiles = [held.tile([P, S], BF16, name=f"base{b}") for b in range(BLOCKS)]
-        nc.sync.dma_start(base_tiles[0][:], base[0:P, :])
-        nc.scalar.dma_start(base_tiles[1][:], base[P : 2 * P, :])
+        for b in range(BLOCKS):
+            nc.scalar.dma_start(base_tiles[b][:], base[b * P : (b + 1) * P, :])
 
-        x_tile = held.tile([P, N], BF16, name="x_tile")
-        nc.scalar.dma_start(x_tile[:], x)
         w_tile = held.tile([P, E, M], BF16, name="w_tile")
         nc.sync.dma_start(w_tile[:], w.rearrange("e k m -> k e m"))
+        x_tile = held.tile([P, N], BF16, name="x_tile")
+        nc.scalar.dma_start(x_tile[:], x)
 
         zeros = held.tile([P, 1], BF16, name="zeros")
         nc.gpsimd.memset(zeros[:], 0.0)
@@ -78,5 +79,5 @@ def tile_scatter_matmul_kernel(tc, base, x, w, c, offs, out):
         for b in range(BLOCKS):
             scaled = held.tile([P, S], F32, name=f"scaled{b}")
             nc.vector.tensor_tensor(scaled[:], window_tiles[b][:], c_tile[:], mybir.AluOpType.mult)
-            store_queue = nc.sync if b == 0 else nc.scalar
+            store_queue = nc.scalar if b == 0 else nc.sync
             store_queue.dma_start(out[b * P : (b + 1) * P, :], scaled[:])

@@ -52,6 +52,9 @@ def tile_scatter_matmul_kernel(tc, base, x, w, c, offs, out):
         ident_f32 = held.tile([P, P], F32, name="ident_f32")
         make_identity(nc, ident_f32[:])
 
+        window_tiles = [windows.tile([P, S], F32, name=f"window{b}") for b in range(BLOCKS)]
+        nc.tensor.matmul(window_tiles[0][:], ident[:], base_tiles[0][:], start=True, stop=True)
+
         c_bank = windows.tile([P, S], F32, name="c_bank")
         for a in range(CPP):
             nc.tensor.transpose(
@@ -62,9 +65,7 @@ def tile_scatter_matmul_kernel(tc, base, x, w, c, offs, out):
             c_tile[:].rearrange("q (p a) -> q p a", a=CPP), c_bank[:].rearrange("q (a p) -> q p a", a=CPP)
         )
 
-        window_tiles = [windows.tile([P, S], F32, name=f"window{b}") for b in range(BLOCKS)]
-        for b in range(BLOCKS):
-            nc.tensor.matmul(window_tiles[b][:], ident[:], base_tiles[b][:], start=True, stop=True)
+        nc.tensor.matmul(window_tiles[1][:], ident[:], base_tiles[1][:], start=True, stop=True)
 
         for b in range(BLOCKS):
             for e in range(E):

@@ -30,9 +30,8 @@ def tile_scatter_matmul_kernel(tc, base, x, w, c, offs, out):
         offsets = held.tile([P, N // 16], U16, name="offsets")
         nc.sync.dma_start(offsets[:], offs)
 
-        base_tiles = [held.tile([P, S], BF16, name=f"base{b}") for b in range(BLOCKS)]
-        for b in range(BLOCKS):
-            nc.scalar.dma_start(base_tiles[b][:], base[b * P : (b + 1) * P, :])
+        base_tile = held.tile([P, BLOCKS, S], BF16, name="base_tile")
+        nc.scalar.dma_start(base_tile[:], base.rearrange("(b p) t -> p b t", p=P))
 
         w_tile = held.tile([P, E, M], BF16, name="w_tile")
         nc.sync.dma_start(w_tile[:], w.rearrange("e k m -> k e m"))
@@ -53,7 +52,7 @@ def tile_scatter_matmul_kernel(tc, base, x, w, c, offs, out):
         make_identity(nc, ident_f32[:])
 
         window_tiles = [windows.tile([P, S], F32, name=f"window{b}") for b in range(BLOCKS)]
-        nc.tensor.matmul(window_tiles[0][:], ident[:], base_tiles[0][:], start=True, stop=True)
+        nc.tensor.matmul(window_tiles[0][:], ident[:], base_tile[:, 0, :], start=True, stop=True)
 
         c_bank = windows.tile([P, S], F32, name="c_bank")
         for a in range(CPP):
@@ -65,7 +64,7 @@ def tile_scatter_matmul_kernel(tc, base, x, w, c, offs, out):
             c_tile[:].rearrange("q (p a) -> q p a", a=CPP), c_bank[:].rearrange("q (a p) -> q p a", a=CPP)
         )
 
-        nc.tensor.matmul(window_tiles[1][:], ident[:], base_tiles[1][:], start=True, stop=True)
+        nc.tensor.matmul(window_tiles[1][:], ident[:], base_tile[:, 1, :], start=True, stop=True)
 
         for b in range(BLOCKS):
             for e in range(E):

@@ -31,12 +31,14 @@ def tile_scatter_matmul_kernel(tc, base, x, w, c, offs, out):
         nc.sync.dma_start(offsets[:], offs)
 
         base_tile = held.tile([P, BLOCKS, S], BF16, name="base_tile")
-        nc.scalar.dma_start(base_tile[:], base.rearrange("(b p) t -> p b t", p=P))
+        nc.sync.dma_start(base_tile[:], base.rearrange("(b p) t -> p b t", p=P))
 
-        w_tile = held.tile([P, E, M], BF16, name="w_tile")
-        nc.sync.dma_start(w_tile[:], w.rearrange("e k m -> k e m"))
         x_tile = held.tile([P, N], BF16, name="x_tile")
-        nc.scalar.dma_start(x_tile[:], x)
+        nc.sync.dma_start(x_tile[:], x)
+
+        w_tiles = [held.tile([P, E, P], BF16, name=f"w{b}") for b in range(BLOCKS)]
+        for b in range(BLOCKS):
+            nc.sync.dma_start(w_tiles[b][:], w[:, :, b * P : (b + 1) * P].rearrange("e k m -> k e m"))
 
         zeros = held.tile([P, 1], BF16, name="zeros")
         nc.gpsimd.memset(zeros[:], 0.0)
@@ -46,13 +48,10 @@ def tile_scatter_matmul_kernel(tc, base, x, w, c, offs, out):
                 warm[:], zeros[:].to_broadcast([P, P]), zeros[:].to_broadcast([P, S]), start=True, stop=True
             )
 
-        ident = held.tile([P, P], BF16, name="ident")
-        make_identity(nc, ident[:])
         ident_f32 = held.tile([P, P], F32, name="ident_f32")
         make_identity(nc, ident_f32[:])
-
-        window_tiles = [windows.tile([P, S], F32, name=f"window{b}") for b in range(BLOCKS)]
-        nc.tensor.matmul(window_tiles[0][:], ident[:], base_tile[:, 0, :], start=True, stop=True)
+        ident = held.tile([P, P], BF16, name="ident")
+        make_identity(nc, ident[:])
 
         c_bank = windows.tile([P, S], F32, name="c_bank")
         for a in range(CPP):
@@ -64,13 +63,15 @@ def tile_scatter_matmul_kernel(tc, base, x, w, c, offs, out):
             c_tile[:].rearrange("q (p a) -> q p a", a=CPP), c_bank[:].rearrange("q (a p) -> q p a", a=CPP)
         )
 
-        nc.tensor.matmul(window_tiles[1][:], ident[:], base_tile[:, 1, :], start=True, stop=True)
+        window_tiles = [windows.tile([P, S], F32, name=f"window{b}") for b in range(BLOCKS)]
+        for b in range(BLOCKS):
+            nc.tensor.matmul(window_tiles[b][:], ident[:], base_tile[:, b, :], start=True, stop=True)
 
         for b in range(BLOCKS):
             for e in range(E):
                 nc.tensor.matmul(
                     window_tiles[b][:].indirect(offsets[:, e * QC : (e + 1) * QC]),
-                    w_tile[:, e, b * P : (b + 1) * P],
+                    w_tiles[b][:, e, :],
                     x_tile[:, e * Q : (e + 1) * Q],
                     start=True,
                     stop=True,

@@ -31,14 +31,14 @@ def tile_scatter_matmul_kernel(tc, base, x, w, c, offs, out):
         nc.sync.dma_start(offsets[:], offs)
 
         base_tile = held.tile([P, BLOCKS, S], BF16, name="base_tile")
-        nc.sync.dma_start(base_tile[:], base.rearrange("(b p) t -> p b t", p=P))
+        nc.scalar.dma_start(base_tile[:], base.rearrange("(b p) t -> p b t", p=P))
 
         x_tile = held.tile([P, N], BF16, name="x_tile")
-        nc.sync.dma_start(x_tile[:], x)
+        nc.scalar.dma_start(x_tile[:], x)
 
         w_tiles = [held.tile([P, E, P], BF16, name=f"w{b}") for b in range(BLOCKS)]
-        for b in range(BLOCKS):
-            nc.sync.dma_start(w_tiles[b][:], w[:, :, b * P : (b + 1) * P].rearrange("e k m -> k e m"))
+        for b, w_queue in enumerate((nc.sync, nc.scalar)):
+            w_queue.dma_start(w_tiles[b][:], w[:, :, b * P : (b + 1) * P].rearrange("e k m -> k e m"))
 
         zeros = held.tile([P, 1], BF16, name="zeros")
         nc.gpsimd.memset(zeros[:], 0.0)

import concourse.mybir as mybir
from concourse.masks import make_identity

BF16, F32, U16 = mybir.dt.bfloat16, mybir.dt.float32, mybir.dt.uint16

P = 128
S = 512
M = 256
N = 384
E = 4
Q = N // E
QC = Q // 16
BLOCKS = M // P
WARM_MATMULS = 4
CPP = S // P

FLOPS = 2 * P * M * N


def tile_scatter_matmul_kernel(tc, base, x, w, c, offs, out):
    nc = tc.nc
    with (
        tc.tile_pool(name="held", bufs=1) as held,
        tc.psum_pool(name="windows", bufs=1) as windows,
    ):

        c_cols = held.tile([P, CPP], F32, name="c_cols")
        nc.sync.dma_start(c_cols[:], c.rearrange("o (p a) -> p (o a)", p=P))

        offsets = held.tile([P, N // 16], U16, name="offsets")
        nc.sync.dma_start(offsets[:], offs)

        base_tile = held.tile([P, BLOCKS, S], BF16, name="base_tile")
        nc.scalar.dma_start(base_tile[:], base.rearrange("(b p) t -> p b t", p=P))

        x_tile = held.tile([P, N], BF16, name="x_tile")
        nc.scalar.dma_start(x_tile[:], x)

        w_tiles = [held.tile([P, E, P], BF16, name=f"w{b}") for b in range(BLOCKS)]
        for b, w_queue in enumerate((nc.sync, nc.scalar)):
            w_queue.dma_start(w_tiles[b][:], w[:, :, b * P : (b + 1) * P].rearrange("e k m -> k e m"))

        zeros = held.tile([P, 1], BF16, name="zeros")
        nc.gpsimd.memset(zeros[:], 0.0)
        warm = windows.tile([P, S], F32, name="warm")
        for i in range(WARM_MATMULS):
            nc.tensor.matmul(
                warm[:], zeros[:].to_broadcast([P, P]), zeros[:].to_broadcast([P, S]), start=True, stop=True
            )

        ident_f32 = held.tile([P, P], F32, name="ident_f32")
        make_identity(nc, ident_f32[:])
        ident = held.tile([P, P], BF16, name="ident")
        make_identity(nc, ident[:])

        c_bank = windows.tile([P, S], F32, name="c_bank")
        for a in range(CPP):
            nc.tensor.transpose(
                c_bank[:, a * P : (a + 1) * P], c_cols[:, a : a + 1].to_broadcast([P, P]), ident_f32[:]
            )
        c_tile = held.tile([P, S], F32, name="c_tile")
        nc.vector.tensor_copy(
            c_tile[:].rearrange("q (p a) -> q p a", a=CPP), c_bank[:].rearrange("q (a p) -> q p a", a=CPP)
        )

        window_tiles = [windows.tile([P, S], F32, name=f"window{b}") for b in range(BLOCKS)]
        for b in range(BLOCKS):
            nc.tensor.matmul(window_tiles[b][:], ident[:], base_tile[:, b, :], start=True, stop=True)

        for b in range(BLOCKS):
            for e in range(E):
                nc.tensor.matmul(
                    window_tiles[b][:].indirect(offsets[:, e * QC : (e + 1) * QC]),
                    w_tiles[b][:, e, :],
                    x_tile[:, e * Q : (e + 1) * Q],
                    start=True,
                    stop=True,
                )

        for b in range(BLOCKS):
            scaled = held.tile([P, S], F32, name=f"scaled{b}")
            nc.vector.tensor_tensor(scaled[:], window_tiles[b][:], c_tile[:], mybir.AluOpType.mult)
            store_queue = nc.scalar if b == 0 else nc.sync
            store_queue.dma_start(out[b * P : (b + 1) * P, :], scaled[:])
